import numpy as np, ml_dtypes
CORES = [16,17,18,19,150,151]
N = 6
GR, GC = 2, 3
L, KA, KB, F = 12, 4, 6, 256
def setup_inputs(rng):
    return {"a": rng.standard_normal((N, 128, KA * 128), dtype=np.float32).astype(ml_dtypes.bfloat16), "b": rng.standard_normal((N, 128, KB * F), dtype=np.float32).astype(ml_dtypes.bfloat16)}
def reference(a, b):
    A, B = a.astype(np.float64), b.astype(np.float64)
    y = np.zeros((N, 128, F))
    for i in range(GR):
        for j in range(GC):
            for k in range(L):
                At = A[i * GC + k // KA][:, 128 * (k % KA):128 * (k % KA) + 128]
                Bt = B[(k // KB) * GC + j][:, F * (k % KB):F * (k % KB) + F]
                y[i * GC + j] += At.T @ Bt
    return {"y": y.astype(ml_dtypes.bfloat16 if a.dtype != np.float64 else np.float64)}

@@ -1,0 +1,214 @@
+from concourse.bass import DstId, RemoteDMATransfer
+from concourse.mybir import AluOpType
+
+N, GR, GC = 6, 2, 3
+L, KA, KB, F, M = 12, 4, 6, 256, 128
+AW, BW = KA * M, KB * F
+
+SCRATCH = {
+    "la": ("sbuf", [128, N * AW], "bfloat16"),
+    "lb": ("sbuf", [128, BW], "bfloat16"),
+    "bx": ("sbuf", [128, 2 * F], "bfloat16"),
+    "ps": ("sbuf", [128, F], "bfloat16"),
+    "pin": ("sbuf", [128, F], "bfloat16"),
+    "ysb": ("sbuf", [128, F], "bfloat16"),
+    "accS": ("psum", [128, 512], "float32"),
+    "accO": ("psum", [128, 512], "float32"),
+}
+SEMAPHORES = ["aload", "bl0", "bl1", "bl2", "arrA0", "arrA1", "arrA2", "arrA3", "arrA4", "arrA5", "arrB", "arrP",
+              "sent", "mmS", "mmO", "evac", "added", "ystore"]
+
+SCHED = {
+    0: [[("A", 1, "near", 1, 0), ("A", 2, "far", 1, 0)],
+        [("B", 3, "all", 1, 0)]],
+    1: [[("A", 4, "far", 2, 0), ("A", 5, "far", 2, 1)],
+        [("A", 3, "near", 2, 0), ("A", 0, "near", 2, 1), ("A", 2, "far", 1, 0)]],
+    2: [[("A", 4, "far", 2, 0), ("A", 5, "far", 2, 1)],
+        [("A", 3, "near", 1, 0)]],
+    3: [[("A", 1, "near", 1, 0), ("A", 2, "far", 1, 0)],
+        [("A", 0, "all", 1, 0)]],
+    4: [[("A", 1, "far", 2, 0), ("A", 2, "far", 2, 1)],
+        [("A", 3, "far", 1, 0)],
+        [("A", 5, "near", 1, 0)]],
+    5: [[("A", 3, "far", 1, 0), ("A", 4, "near", 1, 0)]],
+}
+
+
+def _bits(mask):
+    return [e for e in range(mask.bit_length()) if (mask >> e) & 1]
+
+
+def _plan(cores, topo):
+    def near(x, y):
+        return topo.host(cores[x]) == topo.host(cores[y]) and topo.chip(cores[x]) == topo.chip(cores[y])
+
+    terms = [[] for _ in range(N)]
+    for i in range(GR):
+        for j in range(GC):
+            for k in range(L):
+                ao, bo, yo = i * GC + k // KA, (k // KB) * GC + j, i * GC + j
+                w = yo if (bo != yo and near(bo, yo) and not near(ao, bo)) else bo
+                terms[w].append((i, k))
+    need = {"A": [dict() for _ in range(N)], "B": [dict() for _ in range(N)]}
+    for w in range(N):
+        for (i, k) in terms[w]:
+            for what, s, c, wd in (("A", i * GC + k // KA, M * (k % KA), M), ("B", (k // KB) * GC + w % GC, F * (k % KB), F)):
+                if s != w:
+                    lo, hi = need[what][w].get(s, (c, c + wd))
+                    need[what][w][s] = (min(lo, c), max(hi, c + wd))
+    return near, terms, need
+
+
+def _pools(s, cores, near, topo):
+    far, everything = None, None
+    for d in range(N):
+        if d != s:
+            b = set(_bits(topo.mask(cores[s], cores[d])))
+            if near(s, d):
+                everything = b if everything is None else everything & b
+            else:
+                far = b if far is None else far & b
+    far, everything = sorted(far), sorted(everything)
+    return {"far": far, "near": [e for e in everything if e not in far], "all": everything}
+
+
+def _lanes(s, pool, parts, part, cores, near, topo):
+    p = _pools(s, cores, near, topo)[pool]
+    n = len(p) // parts
+    return p[part * n:(part + 1) * n]
+
+
+def rank_program(g, core, T, topo):
+    r = T.rank_of(core)
+    if r is None:
+        return
+    cores, sem = T.cores, T.sem
+    near, terms, need = _plan(cores, topo)
+
+    def lanes(s, pool, parts, part):
+        return _lanes(s, pool, parts, part, cores, near, topo)
+
+    when, width = {}, {}
+    for s in range(N):
+        for n_call, call in enumerate(SCHED[s]):
+            for (what, d, pool, parts, part) in call:
+                when[(what, s, d)] = n_call
+                width[(what, s, d)] = len(lanes(s, pool, parts, part))
+    for what in ("A", "B"):
+        for d in range(N):
+            for s in need[what][d]:
+                assert (what, s, d) in when
+    assert len(when) == sum(len(need[w][d]) for w in ("A", "B") for d in range(N))
+
+    def p_pool(s, d):
+        return "all" if near(s, d) else "far"
+
+    my_row, col = r // GC, r % GC
+    partner = (1 - my_row) * GC + col
+
+    g.sync.dma_start(T.la[:, r * AW:(r + 1) * AW], T.a[:, :]).then_inc(sem.aload, 16)
+    pieces = sorted(need["B"][d][r] for d in range(N) if r in need["B"][d])
+    at = 0
+    for (lo, hi) in list(pieces):
+        if lo > at:
+            pieces.append((at, lo))
+        at = hi
+    if at < BW:
+        pieces.append((at, BW))
+    for n_piece, (lo, hi) in enumerate(pieces):
+        g.sync.dma_start(T.lb[:, lo:hi], T.b[:, lo:hi]).then_inc(sem["bl%d" % n_piece], 16)
+
+    def b_piece(c):
+        return [n for n, (lo, hi) in enumerate(pieces) if lo <= c < hi][0]
+
+    sent = 0
+    g_waited = set()
+
+    def g_wait(name, val):
+        if name not in g_waited:
+            g_waited.add(name)
+            g.wait_ge(sem[name], val)
+
+    def transfer(d, eng, remote_sem, src, dst):
+        mask = sum(1 << e for e in eng)
+        assert topo.may_write(core, cores[d]) and mask & ~topo.mask(core, cores[d]) == 0
+        rid, pid = topo.addr(cores[d], core)
+        return RemoteDMATransfer(dst_ids=[DstId(rid=rid, pnc=pid)], dma_engine_mask=mask, remote_sem=remote_sem,
+                                 src=src, dst=dst)
+
+    for call in SCHED[r]:
+        trs = []
+        for (what, d, pool, parts, part) in call:
+            lo, hi = need[what][d][r]
+            eng = lanes(r, pool, parts, part)
+            sent += len(eng)
+            if what == "A":
+                g_wait("aload", 16)
+                trs.append(transfer(d, eng, sem["arrA%d" % r], T.la[:, r * AW + lo:r * AW + hi],
+                                    T.la[:, r * AW + lo:r * AW + hi]))
+            else:
+                g_wait("bl%d" % b_piece(lo), 16)
+                trs.append(transfer(d, eng, sem.arrB, T.lb[:, lo:hi], T.bx[:, 0:hi - lo]))
+        g.remote_dma_fused(trs, local_sem=sem.sent)
+
+    def key(s):
+        lo, hi = need["A"][r][s]
+        return (0 if near(s, r) else 1, when[("A", s, r)], hi - lo)
+
+    def steps(i):
+        out = []
+        for s in sorted(set(i * GC + k // KA for (ii, k) in terms[r] if ii == i and i * GC + k // KA != r), key=key):
+            ks = [k for (ii, k) in terms[r] if ii == i and i * GC + k // KA == s]
+            out.extend(sorted(ks, key=lambda k: (0 if (k // KB) * GC + col == r else 1, k)))
+        return out
+
+    own_first = [k for (i, k) in terms[r] if i == my_row and i * GC + k // KA == r]
+    order = ([("O", my_row, k) for k in own_first] + [("S", 1 - my_row, k) for k in steps(1 - my_row)]
+             + [("O", my_row, k) for k in steps(my_row)])
+    assert len(order) == len(terms[r])
+    left = {"S": sum(1 for o in order if o[0] == "S"), "O": sum(1 for o in order if o[0] == "O")}
+    total = dict(left)
+    t_waited = set()
+
+    def t_wait(name, val):
+        if name not in t_waited:
+            t_waited.add(name)
+            g.tensor.wait_ge(sem[name], val)
+
+    for (grp, i, k) in order:
+        s = i * GC + k // KA
+        if s == r:
+            t_wait("aload", 16)
+        else:
+            t_wait("arrA%d" % s, width[("A", s, r)])
+        bo, c = (k // KB) * GC + col, F * (k % KB)
+        if bo == r:
+            t_wait("bl%d" % b_piece(c), 16)
+            rhs = T.lb[:, c:c + F]
+        else:
+            t_wait("arrB", width[("B", bo, r)])
+            off = c - need["B"][r][bo][0]
+            rhs = T.bx[:, off:off + F]
+        acc = T.accS if grp == "S" else T.accO
+        a0 = s * AW + M * (k % KA)
+        first, last = left[grp] == total[grp], left[grp] == 1
+        left[grp] -= 1
+        mm = g.tensor.matmul(acc[:, 0:F], T.la[:, a0:a0 + M], rhs, first, last)
+        if last:
+            mm.then_inc(sem.mmS if grp == "S" else sem.mmO, 1)
+
+    g.vector.wait_ge(sem.mmS, 1)
+    g.vector.tensor_copy(T.ps[:, :], T.accS[:, 0:F]).then_inc(sem.evac, 1)
+    g.wait_ge(sem.evac, 1)
+    eng = lanes(r, p_pool(r, partner), 1, 0)
+    sent += len(eng)
+    g.remote_dma_fused([transfer(partner, eng, sem.arrP, T.ps[:, :], T.pin[:, :])], local_sem=sem.sent)
+
+    g.vector.wait_ge(sem.mmO, 1)
+    g.vector.wait_ge(sem.arrP, len(lanes(partner, p_pool(partner, r), 1, 0)))
+    g.vector.tensor_tensor(T.ysb[:, :], T.accO[:, 0:F], T.pin[:, :], AluOpType.add).then_inc(sem.added, 1)
+    g.sync.wait_ge(sem.added, 1)
+    g.sync.dma_start(T.y[:, :], T.ysb[:, :]).then_inc(sem.ystore, 16)
+
+    g.wait_ge(sem.sent, sent)
+    g.wait_ge(sem.ystore, 16)

@@ -15,22 +15,25 @@ SCRATCH = {
     "accS": ("psum", [128, 512], "float32"),
     "accO": ("psum", [128, 512], "float32"),
 }
-SEMAPHORES = ["aload", "bl0", "bl1", "bl2", "arrA0", "arrA1", "arrA2", "arrA3", "arrA4", "arrA5", "arrB", "arrP",
-              "sent", "mmS", "mmO", "evac", "added", "ystore"]
+SEMAPHORES = ["aload", "bl0", "bl1", "bl2", "arrA0", "arrA1", "arrA2", "arrA3", "arrA4", "arrA5", "rel1", "rel2", "arrB",
+              "arrP", "sent", "mmS", "mmO", "evac", "added", "ystore"]
 
 SCHED = {
-    0: [[("A", 1, "near", 1, 0), ("A", 2, "far", 1, 0)],
-        [("B", 3, "all", 1, 0)]],
-    1: [[("A", 4, "far", 2, 0), ("A", 5, "far", 2, 1)],
-        [("A", 3, "near", 2, 0), ("A", 0, "near", 2, 1), ("A", 2, "far", 1, 0)]],
-    2: [[("A", 4, "far", 2, 0), ("A", 5, "far", 2, 1)],
-        [("A", 3, "near", 1, 0)]],
-    3: [[("A", 1, "near", 1, 0), ("A", 2, "far", 1, 0)],
-        [("A", 0, "all", 1, 0)]],
-    4: [[("A", 1, "far", 2, 0), ("A", 2, "far", 2, 1)],
-        [("A", 3, "far", 1, 0)],
-        [("A", 5, "near", 1, 0)]],
-    5: [[("A", 3, "far", 1, 0), ("A", 4, "near", 1, 0)]],
+    0: [[("A", 0, 0, 4, 1, "near", 1, 0), ("A", 0, 0, 4, 2, "far", 1, 0)],
+        [("B", 0, 4, 6, 3, "all", 1, 0)]],
+    1: [[("A", 1, 2, 4, 4, "far", 1, 0)],
+        [("A", 1, 2, 4, 3, "near", 2, 0), ("A", 1, 0, 2, 0, "near", 2, 1), ("A", 1, 0, 2, 2, "far", 1, 0)]],
+    2: [[("A", 2, 0, 4, 5, "far", 1, 0)],
+        [("A", 2, 0, 4, 3, "near", 1, 0)],
+        [("A", 2, 2, 4, 4, "far", 1, 0)]],
+    3: [[("A", 3, 0, 4, 1, "near", 1, 0), ("A", 3, 0, 4, 2, "far", 1, 0)],
+        [("A", 3, 0, 4, 0, "all", 1, 0)]],
+    4: [[("A", 4, 0, 2, 1, "far", 2, 0), ("A", 4, 0, 2, 2, "far", 2, 1)],
+        [("A", 4, 0, 4, 3, "far", 1, 0)],
+        [("A", 4, 2, 4, 5, "near", 1, 0)],
+        [("A", 1, 2, 4, 5, "all", 1, 0)]],
+    5: [[("A", 5, 0, 4, 3, "far", 1, 0), ("A", 5, 0, 4, 4, "near", 1, 0)],
+        [("A", 2, 0, 2, 4, "all", 1, 0)]],
 }
 
 
@@ -88,17 +91,29 @@ def rank_program(g, core, T, topo):
     def lanes(s, pool, parts, part):
         return _lanes(s, pool, parts, part, cores, near, topo)
 
-    when, width = {}, {}
+    wide = {"A": M, "B": F}
+    land = [dict() for _ in range(N)]
     for s in range(N):
         for n_call, call in enumerate(SCHED[s]):
-            for (what, d, pool, parts, part) in call:
-                when[(what, s, d)] = n_call
-                width[(what, s, d)] = len(lanes(s, pool, parts, part))
-    for what in ("A", "B"):
-        for d in range(N):
-            for s in need[what][d]:
-                assert (what, s, d) in when
-    assert len(when) == sum(len(need[w][d]) for w in ("A", "B") for d in range(N))
+            for (what, blk, t0, t1, d, pool, parts, part) in call:
+                name = "arrB" if what == "B" else ("arrA%d" % blk if blk == s else "rel%d" % blk)
+                land[d][(what, blk, t0 * wide[what], t1 * wide[what])] = (
+                    name, len(lanes(s, pool, parts, part)),
+                    (0 if blk == s else 1, 0 if near(blk, d) else 1, n_call, (t1 - t0) * wide[what]))
+
+    def piece(d, what, blk, c):
+        hit = [(k, v) for k, v in land[d].items() if k[0] == what and k[1] == blk and k[2] <= c < k[3]]
+        assert len(hit) == 1
+        return hit[0]
+
+    for d in range(N):
+        cover = 0
+        for what in ("A", "B"):
+            for blk, (lo, hi) in need[what][d].items():
+                cover += hi - lo
+                for c in range(lo, hi, wide[what]):
+                    piece(d, what, blk, c)
+        assert cover == sum(k[3] - k[2] for k in land[d])
 
     def p_pool(s, d):
         return "all" if near(s, d) else "far"
@@ -138,29 +153,29 @@ def rank_program(g, core, T, topo):
 
     for call in SCHED[r]:
         trs = []
-        for (what, d, pool, parts, part) in call:
-            lo, hi = need[what][d][r]
+        for (what, blk, t0, t1, d, pool, parts, part) in call:
+            lo, hi = t0 * wide[what], t1 * wide[what]
             eng = lanes(r, pool, parts, part)
             sent += len(eng)
+            name = land[d][(what, blk, lo, hi)][0]
             if what == "A":
-                g_wait("aload", 16)
-                trs.append(transfer(d, eng, sem["arrA%d" % r], T.la[:, r * AW + lo:r * AW + hi],
-                                    T.la[:, r * AW + lo:r * AW + hi]))
+                if blk == r:
+                    g_wait("aload", 16)
+                else:
+                    got = piece(r, "A", blk, lo)
+                    assert got[0][3] >= hi
+                    g_wait(got[1][0], got[1][1])
+                trs.append(transfer(d, eng, sem[name], T.la[:, blk * AW + lo:blk * AW + hi],
+                                    T.la[:, blk * AW + lo:blk * AW + hi]))
             else:
                 g_wait("bl%d" % b_piece(lo), 16)
-                trs.append(transfer(d, eng, sem.arrB, T.lb[:, lo:hi], T.bx[:, 0:hi - lo]))
+                trs.append(transfer(d, eng, sem[name], T.lb[:, lo:hi], T.bx[:, 0:hi - lo]))
         g.remote_dma_fused(trs, local_sem=sem.sent)
 
-    def key(s):
-        lo, hi = need["A"][r][s]
-        return (0 if near(s, r) else 1, when[("A", s, r)], hi - lo)
-
     def steps(i):
-        out = []
-        for s in sorted(set(i * GC + k // KA for (ii, k) in terms[r] if ii == i and i * GC + k // KA != r), key=key):
-            ks = [k for (ii, k) in terms[r] if ii == i and i * GC + k // KA == s]
-            out.extend(sorted(ks, key=lambda k: (0 if (k // KB) * GC + col == r else 1, k)))
-        return out
+        ks = [k for (ii, k) in terms[r] if ii == i and i * GC + k // KA != r]
+        return sorted(ks, key=lambda k: (piece(r, "A", i * GC + k // KA, M * (k % KA))[1][2],
+                                         0 if (k // KB) * GC + col == r else 1, k))
 
     own_first = [k for (i, k) in terms[r] if i == my_row and i * GC + k // KA == r]
     order = ([("O", my_row, k) for k in own_first] + [("S", 1 - my_row, k) for k in steps(1 - my_row)]
@@ -180,14 +195,16 @@ def rank_program(g, core, T, topo):
         if s == r:
             t_wait("aload", 16)
         else:
-            t_wait("arrA%d" % s, width[("A", s, r)])
+            got = piece(r, "A", s, M * (k % KA))[1]
+            t_wait(got[0], got[1])
         bo, c = (k // KB) * GC + col, F * (k % KB)
         if bo == r:
             t_wait("bl%d" % b_piece(c), 16)
             rhs = T.lb[:, c:c + F]
         else:
-            t_wait("arrB", width[("B", bo, r)])
-            off = c - need["B"][r][bo][0]
+            got = piece(r, "B", bo, c)
+            t_wait(got[1][0], got[1][1])
+            off = c - got[0][2]
             rhs = T.bx[:, off:off + F]
         acc = T.accS if grp == "S" else T.accO
         a0 = s * AW + M * (k % KA)

from concourse.bass import DstId, RemoteDMATransfer
from concourse.mybir import AluOpType

N, GR, GC = 6, 2, 3
L, KA, KB, F, M = 12, 4, 6, 256, 128
AW, BW = KA * M, KB * F

SCRATCH = {
    "la": ("sbuf", [128, N * AW], "bfloat16"),
    "lb": ("sbuf", [128, BW], "bfloat16"),
    "bx": ("sbuf", [128, 2 * F], "bfloat16"),
    "ps": ("sbuf", [128, F], "bfloat16"),
    "pin": ("sbuf", [128, F], "bfloat16"),
    "ysb": ("sbuf", [128, F], "bfloat16"),
    "accS": ("psum", [128, 512], "float32"),
    "accO": ("psum", [128, 512], "float32"),
}
SEMAPHORES = ["aload", "bl0", "bl1", "bl2", "arrA0", "arrA1", "arrA2", "arrA3", "arrA4", "arrA5", "rel1", "rel2", "arrB",
              "arrP", "sent", "mmS", "mmO", "evac", "added", "ystore"]

SCHED = {
    0: [[("A", 0, 0, 4, 1, "near", 1, 0), ("A", 0, 0, 4, 2, "far", 1, 0)],
        [("B", 0, 4, 6, 3, "all", 1, 0)]],
    1: [[("A", 1, 2, 4, 4, "far", 1, 0)],
        [("A", 1, 2, 4, 3, "near", 2, 0), ("A", 1, 0, 2, 0, "near", 2, 1), ("A", 1, 0, 2, 2, "far", 1, 0)]],
    2: [[("A", 2, 0, 4, 5, "far", 1, 0)],
        [("A", 2, 0, 4, 3, "near", 1, 0)],
        [("A", 2, 2, 4, 4, "far", 1, 0)]],
    3: [[("A", 3, 0, 4, 1, "near", 1, 0), ("A", 3, 0, 4, 2, "far", 1, 0)],
        [("A", 3, 0, 4, 0, "all", 1, 0)]],
    4: [[("A", 4, 0, 2, 1, "far", 2, 0), ("A", 4, 0, 2, 2, "far", 2, 1)],
        [("A", 4, 0, 4, 3, "far", 1, 0)],
        [("A", 4, 2, 4, 5, "near", 1, 0)],
        [("A", 1, 2, 4, 5, "all", 1, 0)]],
    5: [[("A", 5, 0, 4, 3, "far", 1, 0), ("A", 5, 0, 4, 4, "near", 1, 0)],
        [("A", 2, 0, 2, 4, "all", 1, 0)]],
}


def _bits(mask):
    return [e for e in range(mask.bit_length()) if (mask >> e) & 1]


def _plan(cores, topo):
    def near(x, y):
        return topo.host(cores[x]) == topo.host(cores[y]) and topo.chip(cores[x]) == topo.chip(cores[y])

    terms = [[] for _ in range(N)]
    for i in range(GR):
        for j in range(GC):
            for k in range(L):
                ao, bo, yo = i * GC + k // KA, (k // KB) * GC + j, i * GC + j
                w = yo if (bo != yo and near(bo, yo) and not near(ao, bo)) else bo
                terms[w].append((i, k))
    need = {"A": [dict() for _ in range(N)], "B": [dict() for _ in range(N)]}
    for w in range(N):
        for (i, k) in terms[w]:
            for what, s, c, wd in (("A", i * GC + k // KA, M * (k % KA), M), ("B", (k // KB) * GC + w % GC, F * (k % KB), F)):
                if s != w:
                    lo, hi = need[what][w].get(s, (c, c + wd))
                    need[what][w][s] = (min(lo, c), max(hi, c + wd))
    return near, terms, need


def _pools(s, cores, near, topo):
    far, everything = None, None
    for d in range(N):
        if d != s:
            b = set(_bits(topo.mask(cores[s], cores[d])))
            if near(s, d):
                everything = b if everything is None else everything & b
            else:
                far = b if far is None else far & b
    far, everything = sorted(far), sorted(everything)
    return {"far": far, "near": [e for e in everything if e not in far], "all": everything}


def _lanes(s, pool, parts, part, cores, near, topo):
    p = _pools(s, cores, near, topo)[pool]
    n = len(p) // parts
    return p[part * n:(part + 1) * n]


def rank_program(g, core, T, topo):
    r = T.rank_of(core)
    if r is None:
        return
    cores, sem = T.cores, T.sem
    near, terms, need = _plan(cores, topo)

    def lanes(s, pool, parts, part):
        return _lanes(s, pool, parts, part, cores, near, topo)

    wide = {"A": M, "B": F}
    land = [dict() for _ in range(N)]
    for s in range(N):
        for n_call, call in enumerate(SCHED[s]):
            for (what, blk, t0, t1, d, pool, parts, part) in call:
                name = "arrB" if what == "B" else ("arrA%d" % blk if blk == s else "rel%d" % blk)
                land[d][(what, blk, t0 * wide[what], t1 * wide[what])] = (
                    name, len(lanes(s, pool, parts, part)),
                    (0 if blk == s else 1, 0 if near(blk, d) else 1, n_call, (t1 - t0) * wide[what]))

    def piece(d, what, blk, c):
        hit = [(k, v) for k, v in land[d].items() if k[0] == what and k[1] == blk and k[2] <= c < k[3]]
        assert len(hit) == 1
        return hit[0]

    for d in range(N):
        cover = 0
        for what in ("A", "B"):
            for blk, (lo, hi) in need[what][d].items():
                cover += hi - lo
                for c in range(lo, hi, wide[what]):
                    piece(d, what, blk, c)
        assert cover == sum(k[3] - k[2] for k in land[d])

    def p_pool(s, d):
        return "all" if near(s, d) else "far"

    my_row, col = r // GC, r % GC
    partner = (1 - my_row) * GC + col

    g.sync.dma_start(T.la[:, r * AW:(r + 1) * AW], T.a[:, :]).then_inc(sem.aload, 16)
    pieces = sorted(need["B"][d][r] for d in range(N) if r in need["B"][d])
    at = 0
    for (lo, hi) in list(pieces):
        if lo > at:
            pieces.append((at, lo))
        at = hi
    if at < BW:
        pieces.append((at, BW))
    for n_piece, (lo, hi) in enumerate(pieces):
        g.sync.dma_start(T.lb[:, lo:hi], T.b[:, lo:hi]).then_inc(sem["bl%d" % n_piece], 16)

    def b_piece(c):
        return [n for n, (lo, hi) in enumerate(pieces) if lo <= c < hi][0]

    sent = 0
    g_waited = set()

    def g_wait(name, val):
        if name not in g_waited:
            g_waited.add(name)
            g.wait_ge(sem[name], val)

    def transfer(d, eng, remote_sem, src, dst):
        mask = sum(1 << e for e in eng)
        assert topo.may_write(core, cores[d]) and mask & ~topo.mask(core, cores[d]) == 0
        rid, pid = topo.addr(cores[d], core)
        return RemoteDMATransfer(dst_ids=[DstId(rid=rid, pnc=pid)], dma_engine_mask=mask, remote_sem=remote_sem,
                                 src=src, dst=dst)

    for call in SCHED[r]:
        trs = []
        for (what, blk, t0, t1, d, pool, parts, part) in call:
            lo, hi = t0 * wide[what], t1 * wide[what]
            eng = lanes(r, pool, parts, part)
            sent += len(eng)
            name = land[d][(what, blk, lo, hi)][0]
            if what == "A":
                if blk == r:
                    g_wait("aload", 16)
                else:
                    got = piece(r, "A", blk, lo)
                    assert got[0][3] >= hi
                    g_wait(got[1][0], got[1][1])
                trs.append(transfer(d, eng, sem[name], T.la[:, blk * AW + lo:blk * AW + hi],
                                    T.la[:, blk * AW + lo:blk * AW + hi]))
            else:
                g_wait("bl%d" % b_piece(lo), 16)
                trs.append(transfer(d, eng, sem[name], T.lb[:, lo:hi], T.bx[:, 0:hi - lo]))
        g.remote_dma_fused(trs, local_sem=sem.sent)

    def steps(i):
        ks = [k for (ii, k) in terms[r] if ii == i and i * GC + k // KA != r]
        return sorted(ks, key=lambda k: (piece(r, "A", i * GC + k // KA, M * (k % KA))[1][2],
                                         0 if (k // KB) * GC + col == r else 1, k))

    own_first = [k for (i, k) in terms[r] if i == my_row and i * GC + k // KA == r]
    order = ([("O", my_row, k) for k in own_first] + [("S", 1 - my_row, k) for k in steps(1 - my_row)]
             + [("O", my_row, k) for k in steps(my_row)])
    assert len(order) == len(terms[r])
    left = {"S": sum(1 for o in order if o[0] == "S"), "O": sum(1 for o in order if o[0] == "O")}
    total = dict(left)
    t_waited = set()

    def t_wait(name, val):
        if name not in t_waited:
            t_waited.add(name)
            g.tensor.wait_ge(sem[name], val)

    for (grp, i, k) in order:
        s = i * GC + k // KA
        if s == r:
            t_wait("aload", 16)
        else:
            got = piece(r, "A", s, M * (k % KA))[1]
            t_wait(got[0], got[1])
        bo, c = (k // KB) * GC + col, F * (k % KB)
        if bo == r:
            t_wait("bl%d" % b_piece(c), 16)
            rhs = T.lb[:, c:c + F]
        else:
            got = piece(r, "B", bo, c)
            t_wait(got[1][0], got[1][1])
            off = c - got[0][2]
            rhs = T.bx[:, off:off + F]
        acc = T.accS if grp == "S" else T.accO
        a0 = s * AW + M * (k % KA)
        first, last = left[grp] == total[grp], left[grp] == 1
        left[grp] -= 1
        mm = g.tensor.matmul(acc[:, 0:F], T.la[:, a0:a0 + M], rhs, first, last)
        if last:
            mm.then_inc(sem.mmS if grp == "S" else sem.mmO, 1)

    g.vector.wait_ge(sem.mmS, 1)
    g.vector.tensor_copy(T.ps[:, :], T.accS[:, 0:F]).then_inc(sem.evac, 1)
    g.wait_ge(sem.evac, 1)
    eng = lanes(r, p_pool(r, partner), 1, 0)
    sent += len(eng)
    g.remote_dma_fused([transfer(partner, eng, sem.arrP, T.ps[:, :], T.pin[:, :])], local_sem=sem.sent)

    g.vector.wait_ge(sem.mmO, 1)
    g.vector.wait_ge(sem.arrP, len(lanes(partner, p_pool(partner, r), 1, 0)))
    g.vector.tensor_tensor(T.ysb[:, :], T.accO[:, 0:F], T.pin[:, :], AluOpType.add).then_inc(sem.added, 1)
    g.sync.wait_ge(sem.added, 1)
    g.sync.dma_start(T.y[:, :], T.ysb[:, :]).then_inc(sem.ystore, 16)

    g.wait_ge(sem.sent, sent)
    g.wait_ge(sem.ystore, 16)
